import numpy as np
import ml_dtypes


def mxq(x, axis, fmt="e4m3"):
    dtype, down = {"e4m3": (ml_dtypes.float8_e4m3fn, 7), "e5m2": (ml_dtypes.float8_e5m2, 14)}[fmt]
    v = np.moveaxis(np.asarray(x, np.float32).astype(ml_dtypes.bfloat16).astype(np.float64), axis, -1)
    blocks = v.reshape(v.shape[:-1] + (-1, 32))
    amax = np.abs(blocks).max(-1, keepdims=True)
    byte = np.maximum(np.where(amax > 0, np.frexp(amax)[1] - 1 + 127, 0) - down, 1)
    scale = np.exp2(byte - 127.0)
    codes = (blocks / scale).astype(np.float32).astype(dtype).astype(np.float64)
    return np.moveaxis((codes * scale).reshape(v.shape), -1, axis)


WIDE = False


def mx_kscale(k):
    if not WIDE:
        return np.ones(k)
    levels = np.array([10, -10, 5, -5, 0])
    if k % 512:
        return np.exp2(np.random.permutation(np.resize(levels, k // 32))).repeat(32)
    a = np.empty((k // 512, 16))
    for p in range(k // 512):
        a[p, :8] = np.random.permutation(np.resize(levels, 8))
        for g in range(8):
            far = levels[np.abs(levels - a[p, g]) >= 10]
            a[p, g + 8] = far[np.random.randint(len(far))]
    return np.exp2(a.ravel()).repeat(32)


def f64(x):
    return np.asarray(x).astype(np.float64)


def striped(idx):
    return np.tile(idx.reshape(-1, 16).T, (8, 1)).astype(np.uint16)


def unstriped(offs):
    return offs[:16].T.reshape(-1).astype(np.int64)


def gelu(v):
    return 0.5 * v * (1.0 + np.tanh(np.sqrt(2.0 / np.pi) * (v + 0.044715 * v**3)))


K, T, D, S, V, H, N = 512, 1024, 4, 1024, 256, 1024, 256


def setup_inputs():
    n = np.random.standard_normal
    s = mx_kscale(K)[:, None]
    u = mx_kscale(H)
    return {
        "xT": (n((K, T)) * s).astype(np.float32),
        "w1": (n((K, H)) / np.sqrt(K) / s * u).astype(np.float32),
        "w2": (n((H, N)) / np.sqrt(H) / u[:, None]).astype(np.float32),
        "offs": striped(np.concatenate([np.random.permutation(T)[:V] for _ in range(D)])),
    }


def reference(xT, w1, w2, offs):
    idx = unstriped(offs)
    x = np.empty((K, V))
    for l in range(D):
        r = l // 4 * (4 * K // D) + l % 4 + 4 * np.arange(K // D)
        x[r] = f64(xT)[r][:, idx[l * V:(l + 1) * V]]
    xq = mxq(x, 0, "e4m3")
    h = gelu(mxq(f64(w1), 0, "e4m3").T @ xq)
    return mxq(f64(w2), 0, "e4m3").T @ mxq(h, 0, "e4m3")

@@ -1,0 +1,135 @@
+from contextlib import ExitStack
+
+import concourse.mybir as mybir
+
+F32 = mybir.dt.float32
+BF16 = mybir.dt.bfloat16
+U32 = mybir.dt.uint32
+U16 = mybir.dt.uint16
+U8 = mybir.dt.uint8
+FP8X4 = mybir.dt.float8_e4m3fn_x4
+GELU = mybir.ActivationFunctionType.Gelu_apprx_tanh
+P = 128
+K, T, H, N, V, L = 512, 1024, 1024, 256, 256, 4
+FLOPS = 2 * V * (K * H + H * N)
+
+
+def tile_picked_grid_mlp_gelu_sub_l_kernel(tc, xT, w1, w2, offs, out):
+    nc = tc.nc
+    with ExitStack() as ctx:
+        held = ctx.enter_context(tc.tile_pool(name="held", bufs=1))
+        psum = ctx.enter_context(tc.psum_pool(name="psum", bufs=1))
+
+        offsets = held.tile([P, L * V // 16], U16, name="offsets")
+        level = [held.tile([P, T], F32, name="level%d" % l) for l in range(L)]
+        w1a_raw = held.tile([P, 4, 512], F32, name="w1a_raw")
+        w1b_raw = [held.tile([P, 4, 256], F32, name="w1b_raw%d" % i) for i in range(2)]
+        w2_raw = [held.tile([P, 4, N], F32, name="w2_raw%d" % g) for g in range(2)]
+
+        x_bf = held.tile([P, V, 4], BF16, name="x_bf", align_bytes=64)
+        x_codes = held.tile([P, V], U32, name="x_codes", align_bytes=64)
+        x_scales = held.tile([P, V], U8, name="x_scales", align_bytes=64)
+        w1_bf = [held.tile([P, 4, P, 4], BF16, name="w1_bf%d" % g, align_bytes=64) for g in range(2)]
+        w1_codes = [held.tile([P, 512], U32, name="w1_codes%d" % g, align_bytes=64) for g in range(2)]
+        w1_scales = [held.tile([P, 512], U8, name="w1_scales%d" % g, align_bytes=64) for g in range(2)]
+        w2_bf = [held.tile([P, N, 4], BF16, name="w2_bf%d" % g, align_bytes=64) for g in range(2)]
+        w2_codes = [held.tile([P, N], U32, name="w2_codes%d" % g, align_bytes=64) for g in range(2)]
+        w2_scales = [held.tile([P, N], U8, name="w2_scales%d" % g, align_bytes=64) for g in range(2)]
+        h_bf = [[held.tile([P, P, 4], BF16, name="h_bf%d%d" % (g, n), align_bytes=64) for n in range(2)] for g in range(2)]
+        h_codes = [[held.tile([P, P], U32, name="h_codes%d%d" % (g, n), align_bytes=64) for n in range(2)] for g in range(2)]
+        h_scales = [[held.tile([P, P], U8, name="h_scales%d%d" % (g, n), align_bytes=64) for n in range(2)] for g in range(2)]
+        out_sb = [[held.tile([P, P], F32, name="out_sb%d%d" % (m, n)) for n in range(2)] for m in range(2)]
+        h_ps = [[psum.tile([P, 4, P], F32, name="h_ps%d%d" % (g, n)) for n in range(2)] for g in range(2)]
+        out_ps = [[psum.tile([P, 512], F32, name="out_ps%d%d" % (m, n)) for n in range(2)] for m in range(2)]
+        warm = held.tile([P, 2], F32, name="warm")
+
+        w1_rows = w1.rearrange("(p j) c -> p j c", j=4)
+        w2_rows = w2.rearrange("(g p j) c -> g p j c", g=2, j=4)
+        x_rows = xT.rearrange("(p l) c -> l p c", l=4)
+
+        nc.sync.dma_start(offsets[:], offs)
+        nc.sync.dma_start(w1a_raw[:], w1_rows[:, :, 0:512])
+        for l in range(L):
+            nc.sync.dma_start(level[l][:], x_rows[l])
+        for i in range(2):
+            nc.sync.dma_start(w1b_raw[i][:], w1_rows[:, :, 512 + 256 * i : 768 + 256 * i])
+        for g in range(2):
+            nc.sync.dma_start(w2_raw[g][:], w2_rows[g])
+
+        nc.vector.memset(warm[:], 0.0)
+        nc.scalar.activation(warm[:, 1:2], warm[:, 0:1], GELU)
+
+        def cast_w1(copy, g, raw, m0, lo, hi):
+            copy(w1_bf[g][:].rearrange("p t m j -> p m t j")[:, m0 + lo : m0 + hi], raw[:].rearrange("p j (m t) -> p m t j", t=4)[:, lo:hi])
+
+        def quantise_w1(g, half):
+            w = slice(256 * half, 256 * half + 256)
+            nc.vector.quantize_mx(
+                out=w1_codes[g][:, w].bitcast(FP8X4),
+                scales=w1_scales[g][:, w],
+                in_=w1_bf[g][:].rearrange("p t m j -> p (t m j)")[:, 1024 * half : 1024 * half + 1024],
+            )
+
+        def cast_w2(copy, g, lo, hi):
+            copy(w2_bf[g][:, lo:hi, :], w2_raw[g][:].rearrange("p j c -> p c j")[:, lo:hi])
+
+        def quantise(codes, scales, src):
+            nc.vector.quantize_mx(out=codes[:].bitcast(FP8X4), scales=scales[:], in_=src[:].rearrange("p n j -> p (n j)"))
+
+        def layer1(g, n):
+            v = slice(P * n, P * n + P)
+            for t in range(4):
+                m = slice(P * t, P * t + P)
+                nc.tensor.matmul_mx(
+                    out=h_ps[g][n][:, t, :],
+                    lhsT=w1_codes[g][:, m].bitcast(FP8X4),
+                    lhsT_scale=w1_scales[g][:, m],
+                    rhs=x_codes[:, v].bitcast(FP8X4),
+                    rhs_scale=x_scales[:, v],
+                    start=True,
+                    stop=True,
+                )
+            nc.scalar.activation(h_bf[g][n][:], h_ps[g][n][:].rearrange("p t n -> p n t"), GELU)
+
+        def layer2(g, n):
+            for mt in range(2):
+                m = slice(P * mt, P * mt + P)
+                nc.tensor.matmul_mx(
+                    out=out_ps[mt][n][:, 0:P],
+                    lhsT=w2_codes[g][:, m].bitcast(FP8X4),
+                    lhsT_scale=w2_scales[g][:, m],
+                    rhs=h_codes[g][n][:].bitcast(FP8X4),
+                    rhs_scale=h_scales[g][n][:],
+                    start=(g == 0),
+                    stop=(g == 1),
+                )
+
+        cast_w1(nc.vector.tensor_copy, 0, w1a_raw, 0, 0, 64)
+        cast_w1(nc.scalar.copy, 0, w1a_raw, 0, 64, 128)
+        for half in range(2):
+            quantise_w1(0, half)
+        for l in range(L):
+            nc.vector.tensor_copy(x_bf[:, :, l], level[l][:].indirect(offsets[:, 16 * l : 16 * l + 16]))
+        quantise(x_codes, x_scales, x_bf)
+        for n in range(2):
+            layer1(0, n)
+        for i in range(2):
+            cast_w1(nc.vector.tensor_copy, 1, w1b_raw[i], 64 * i, 0, 64)
+        for half in range(2):
+            quantise_w1(1, half)
+        for n in range(2):
+            layer1(1, n)
+            quantise(h_codes[0][n], h_scales[0][n], h_bf[0][n])
+        for g in range(2):
+            cast_w2(nc.vector.tensor_copy, g, 0, 128)
+            cast_w2(nc.scalar.copy, g, 128, 256)
+            quantise(w2_codes[g], w2_scales[g], w2_bf[g])
+        for n in range(2):
+            layer2(0, n)
+        for n in range(2):
+            quantise(h_codes[1][n], h_scales[1][n], h_bf[1][n])
+            layer2(1, n)
+            nc.vector.tensor_copy(out_sb[0][n][:], out_ps[0][n][:, 0:P])
+            nc.scalar.copy(out_sb[1][n][:], out_ps[1][n][:, 0:P])
+            nc.sync.dma_start(out[0:P, P * n : P * n + P], out_sb[0][n][:])
+            nc.scalar.dma_start(out[P : 2 * P, P * n : P * n + P], out_sb[1][n][:])

@@ -23,21 +23,23 @@ def tile_picked_grid_mlp_gelu_sub_l_kernel(tc, xT, w1, w2, offs, out):
         offsets = held.tile([P, L * V // 16], U16, name="offsets")
         level = [held.tile([P, T], F32, name="level%d" % l) for l in range(L)]
         w1a_raw = held.tile([P, 4, 512], F32, name="w1a_raw")
-        w1b_raw = [held.tile([P, 4, 256], F32, name="w1b_raw%d" % i) for i in range(2)]
+        w1b_raw = [held.tile([P, 2, 512], F32, name="w1b_raw%d" % i) for i in range(2)]
         w2_raw = [held.tile([P, 4, N], F32, name="w2_raw%d" % g) for g in range(2)]
 
         x_bf = held.tile([P, V, 4], BF16, name="x_bf", align_bytes=64)
         x_codes = held.tile([P, V], U32, name="x_codes", align_bytes=64)
         x_scales = held.tile([P, V], U8, name="x_scales", align_bytes=64)
-        w1_bf = [held.tile([P, 4, P, 4], BF16, name="w1_bf%d" % g, align_bytes=64) for g in range(2)]
+        w1_store = [held.tile([P, 1024], U32, name="w1_store%d" % g, align_bytes=64) for g in range(2)]
+        w1_bf = [w1_store[g][:].bitcast(BF16) for g in range(2)]
         w1_codes = [held.tile([P, 512], U32, name="w1_codes%d" % g, align_bytes=64) for g in range(2)]
         w1_scales = [held.tile([P, 512], U8, name="w1_scales%d" % g, align_bytes=64) for g in range(2)]
-        w2_bf = [held.tile([P, N, 4], BF16, name="w2_bf%d" % g, align_bytes=64) for g in range(2)]
         w2_codes = [held.tile([P, N], U32, name="w2_codes%d" % g, align_bytes=64) for g in range(2)]
         w2_scales = [held.tile([P, N], U8, name="w2_scales%d" % g, align_bytes=64) for g in range(2)]
         h_bf = [[held.tile([P, P, 4], BF16, name="h_bf%d%d" % (g, n), align_bytes=64) for n in range(2)] for g in range(2)]
-        h_codes = [[held.tile([P, P], U32, name="h_codes%d%d" % (g, n), align_bytes=64) for n in range(2)] for g in range(2)]
-        h_scales = [[held.tile([P, P], U8, name="h_scales%d%d" % (g, n), align_bytes=64) for n in range(2)] for g in range(2)]
+        h_own = [held.tile([P, P], U32, name="h_codes%d" % n, align_bytes=64) for n in range(2)]
+        h_codes = [[x_codes[:, P * n : P * n + P] for n in range(2)], [h_own[n][:] for n in range(2)]]
+        h_own_scales = [held.tile([P, P], U8, name="h_scales%d" % n, align_bytes=64) for n in range(2)]
+        h_scales = [[x_scales[:, P * n : P * n + P] for n in range(2)], [h_own_scales[n][:] for n in range(2)]]
         out_sb = [[held.tile([P, P], F32, name="out_sb%d%d" % (m, n)) for n in range(2)] for m in range(2)]
         h_ps = [[psum.tile([P, 4, P], F32, name="h_ps%d%d" % (g, n)) for n in range(2)] for g in range(2)]
         out_ps = [[psum.tile([P, 512], F32, name="out_ps%d%d" % (m, n)) for n in range(2)] for m in range(2)]
@@ -52,29 +54,34 @@ def tile_picked_grid_mlp_gelu_sub_l_kernel(tc, xT, w1, w2, offs, out):
         for l in range(L):
             nc.sync.dma_start(level[l][:], x_rows[l])
         for i in range(2):
-            nc.sync.dma_start(w1b_raw[i][:], w1_rows[:, :, 512 + 256 * i : 768 + 256 * i])
+            nc.sync.dma_start(w1b_raw[i][:], w1_rows[:, 2 * i : 2 * i + 2, 512:1024])
         for g in range(2):
             nc.sync.dma_start(w2_raw[g][:], w2_rows[g])
 
         nc.vector.memset(warm[:], 0.0)
         nc.scalar.activation(warm[:, 1:2], warm[:, 0:1], GELU)
 
-        def cast_w1(copy, g, raw, m0, lo, hi):
-            copy(w1_bf[g][:].rearrange("p t m j -> p m t j")[:, m0 + lo : m0 + hi], raw[:].rearrange("p j (m t) -> p m t j", t=4)[:, lo:hi])
+        def cast_w1(copy, g, j0, raw, lo, hi):
+            copy(
+                w1_bf[g].rearrange("p (t m j) -> p m t j", t=4, j=4)[:, lo:hi, :, j0 : j0 + raw.shape[1]],
+                raw[:].rearrange("p j (m t) -> p m t j", t=4)[:, lo:hi],
+            )
 
         def quantise_w1(g, half):
             w = slice(256 * half, 256 * half + 256)
             nc.vector.quantize_mx(
                 out=w1_codes[g][:, w].bitcast(FP8X4),
                 scales=w1_scales[g][:, w],
-                in_=w1_bf[g][:].rearrange("p t m j -> p (t m j)")[:, 1024 * half : 1024 * half + 1024],
+                in_=w1_bf[g][:, 1024 * half : 1024 * half + 1024],
             )
 
-        def cast_w2(copy, g, lo, hi):
-            copy(w2_bf[g][:, lo:hi, :], w2_raw[g][:].rearrange("p j c -> p c j")[:, lo:hi])
+        def prepare_w2(g):
+            grouped = w1_bf[1 - g][:, 0:1024]
+            nc.vector.tensor_copy(grouped.rearrange("p (c j) -> p c j", j=4), w2_raw[g][:].rearrange("p j c -> p c j"))
+            nc.vector.quantize_mx(out=w2_codes[g][:].bitcast(FP8X4), scales=w2_scales[g][:], in_=grouped)
 
         def quantise(codes, scales, src):
-            nc.vector.quantize_mx(out=codes[:].bitcast(FP8X4), scales=scales[:], in_=src[:].rearrange("p n j -> p (n j)"))
+            nc.vector.quantize_mx(out=codes.bitcast(FP8X4), scales=scales, in_=src[:].rearrange("p n j -> p (n j)"))
 
         def layer1(g, n):
             v = slice(P * n, P * n + P)
@@ -98,32 +105,31 @@ def tile_picked_grid_mlp_gelu_sub_l_kernel(tc, xT, w1, w2, offs, out):
                     out=out_ps[mt][n][:, 0:P],
                     lhsT=w2_codes[g][:, m].bitcast(FP8X4),
                     lhsT_scale=w2_scales[g][:, m],
-                    rhs=h_codes[g][n][:].bitcast(FP8X4),
-                    rhs_scale=h_scales[g][n][:],
+                    rhs=h_codes[g][n].bitcast(FP8X4),
+                    rhs_scale=h_scales[g][n],
                     start=(g == 0),
                     stop=(g == 1),
                 )
 
-        cast_w1(nc.vector.tensor_copy, 0, w1a_raw, 0, 0, 64)
-        cast_w1(nc.scalar.copy, 0, w1a_raw, 0, 64, 128)
+        cast_w1(nc.vector.tensor_copy, 0, 0, w1a_raw, 0, 72)
+        cast_w1(nc.scalar.copy, 0, 0, w1a_raw, 72, 128)
         for half in range(2):
             quantise_w1(0, half)
         for l in range(L):
             nc.vector.tensor_copy(x_bf[:, :, l], level[l][:].indirect(offsets[:, 16 * l : 16 * l + 16]))
-        quantise(x_codes, x_scales, x_bf)
+        quantise(x_codes[:], x_scales[:], x_bf)
         for n in range(2):
             layer1(0, n)
         for i in range(2):
-            cast_w1(nc.vector.tensor_copy, 1, w1b_raw[i], 64 * i, 0, 64)
+            cast_w1(nc.vector.tensor_copy, 1, 2 * i, w1b_raw[i], 0, 128)
         for half in range(2):
             quantise_w1(1, half)
         for n in range(2):
             layer1(1, n)
+        for n in range(2):
             quantise(h_codes[0][n], h_scales[0][n], h_bf[0][n])
         for g in range(2):
-            cast_w2(nc.vector.tensor_copy, g, 0, 128)
-            cast_w2(nc.scalar.copy, g, 128, 256)
-            quantise(w2_codes[g], w2_scales[g], w2_bf[g])
+            prepare_w2(g)
         for n in range(2):
             layer2(0, n)
         for n in range(2):

from contextlib import ExitStack

import concourse.mybir as mybir

F32 = mybir.dt.float32
BF16 = mybir.dt.bfloat16
U32 = mybir.dt.uint32
U16 = mybir.dt.uint16
U8 = mybir.dt.uint8
FP8X4 = mybir.dt.float8_e4m3fn_x4
GELU = mybir.ActivationFunctionType.Gelu_apprx_tanh
P = 128
K, T, H, N, V, L = 512, 1024, 1024, 256, 256, 4
FLOPS = 2 * V * (K * H + H * N)


def tile_picked_grid_mlp_gelu_sub_l_kernel(tc, xT, w1, w2, offs, out):
    nc = tc.nc
    with ExitStack() as ctx:
        held = ctx.enter_context(tc.tile_pool(name="held", bufs=1))
        psum = ctx.enter_context(tc.psum_pool(name="psum", bufs=1))

        offsets = held.tile([P, L * V // 16], U16, name="offsets")
        level = [held.tile([P, T], F32, name="level%d" % l) for l in range(L)]
        w1a_raw = held.tile([P, 4, 512], F32, name="w1a_raw")
        w1b_raw = [held.tile([P, 2, 512], F32, name="w1b_raw%d" % i) for i in range(2)]
        w2_raw = [held.tile([P, 4, N], F32, name="w2_raw%d" % g) for g in range(2)]

        x_bf = held.tile([P, V, 4], BF16, name="x_bf", align_bytes=64)
        x_codes = held.tile([P, V], U32, name="x_codes", align_bytes=64)
        x_scales = held.tile([P, V], U8, name="x_scales", align_bytes=64)
        w1_store = [held.tile([P, 1024], U32, name="w1_store%d" % g, align_bytes=64) for g in range(2)]
        w1_bf = [w1_store[g][:].bitcast(BF16) for g in range(2)]
        w1_codes = [held.tile([P, 512], U32, name="w1_codes%d" % g, align_bytes=64) for g in range(2)]
        w1_scales = [held.tile([P, 512], U8, name="w1_scales%d" % g, align_bytes=64) for g in range(2)]
        w2_codes = [held.tile([P, N], U32, name="w2_codes%d" % g, align_bytes=64) for g in range(2)]
        w2_scales = [held.tile([P, N], U8, name="w2_scales%d" % g, align_bytes=64) for g in range(2)]
        h_bf = [[held.tile([P, P, 4], BF16, name="h_bf%d%d" % (g, n), align_bytes=64) for n in range(2)] for g in range(2)]
        h_own = [held.tile([P, P], U32, name="h_codes%d" % n, align_bytes=64) for n in range(2)]
        h_codes = [[x_codes[:, P * n : P * n + P] for n in range(2)], [h_own[n][:] for n in range(2)]]
        h_own_scales = [held.tile([P, P], U8, name="h_scales%d" % n, align_bytes=64) for n in range(2)]
        h_scales = [[x_scales[:, P * n : P * n + P] for n in range(2)], [h_own_scales[n][:] for n in range(2)]]
        out_sb = [[held.tile([P, P], F32, name="out_sb%d%d" % (m, n)) for n in range(2)] for m in range(2)]
        h_ps = [[psum.tile([P, 4, P], F32, name="h_ps%d%d" % (g, n)) for n in range(2)] for g in range(2)]
        out_ps = [[psum.tile([P, 512], F32, name="out_ps%d%d" % (m, n)) for n in range(2)] for m in range(2)]
        warm = held.tile([P, 2], F32, name="warm")

        w1_rows = w1.rearrange("(p j) c -> p j c", j=4)
        w2_rows = w2.rearrange("(g p j) c -> g p j c", g=2, j=4)
        x_rows = xT.rearrange("(p l) c -> l p c", l=4)

        nc.sync.dma_start(offsets[:], offs)
        nc.sync.dma_start(w1a_raw[:], w1_rows[:, :, 0:512])
        for l in range(L):
            nc.sync.dma_start(level[l][:], x_rows[l])
        for i in range(2):
            nc.sync.dma_start(w1b_raw[i][:], w1_rows[:, 2 * i : 2 * i + 2, 512:1024])
        for g in range(2):
            nc.sync.dma_start(w2_raw[g][:], w2_rows[g])

        nc.vector.memset(warm[:], 0.0)
        nc.scalar.activation(warm[:, 1:2], warm[:, 0:1], GELU)

        def cast_w1(copy, g, j0, raw, lo, hi):
            copy(
                w1_bf[g].rearrange("p (t m j) -> p m t j", t=4, j=4)[:, lo:hi, :, j0 : j0 + raw.shape[1]],
                raw[:].rearrange("p j (m t) -> p m t j", t=4)[:, lo:hi],
            )

        def quantise_w1(g, half):
            w = slice(256 * half, 256 * half + 256)
            nc.vector.quantize_mx(
                out=w1_codes[g][:, w].bitcast(FP8X4),
                scales=w1_scales[g][:, w],
                in_=w1_bf[g][:, 1024 * half : 1024 * half + 1024],
            )

        def prepare_w2(g):
            grouped = w1_bf[1 - g][:, 0:1024]
            nc.vector.tensor_copy(grouped.rearrange("p (c j) -> p c j", j=4), w2_raw[g][:].rearrange("p j c -> p c j"))
            nc.vector.quantize_mx(out=w2_codes[g][:].bitcast(FP8X4), scales=w2_scales[g][:], in_=grouped)

        def quantise(codes, scales, src):
            nc.vector.quantize_mx(out=codes.bitcast(FP8X4), scales=scales, in_=src[:].rearrange("p n j -> p (n j)"))

        def layer1(g, n):
            v = slice(P * n, P * n + P)
            for t in range(4):
                m = slice(P * t, P * t + P)
                nc.tensor.matmul_mx(
                    out=h_ps[g][n][:, t, :],
                    lhsT=w1_codes[g][:, m].bitcast(FP8X4),
                    lhsT_scale=w1_scales[g][:, m],
                    rhs=x_codes[:, v].bitcast(FP8X4),
                    rhs_scale=x_scales[:, v],
                    start=True,
                    stop=True,
                )
            nc.scalar.activation(h_bf[g][n][:], h_ps[g][n][:].rearrange("p t n -> p n t"), GELU)

        def layer2(g, n):
            for mt in range(2):
                m = slice(P * mt, P * mt + P)
                nc.tensor.matmul_mx(
                    out=out_ps[mt][n][:, 0:P],
                    lhsT=w2_codes[g][:, m].bitcast(FP8X4),
                    lhsT_scale=w2_scales[g][:, m],
                    rhs=h_codes[g][n].bitcast(FP8X4),
                    rhs_scale=h_scales[g][n],
                    start=(g == 0),
                    stop=(g == 1),
                )

        cast_w1(nc.vector.tensor_copy, 0, 0, w1a_raw, 0, 72)
        cast_w1(nc.scalar.copy, 0, 0, w1a_raw, 72, 128)
        for half in range(2):
            quantise_w1(0, half)
        for l in range(L):
            nc.vector.tensor_copy(x_bf[:, :, l], level[l][:].indirect(offsets[:, 16 * l : 16 * l + 16]))
        quantise(x_codes[:], x_scales[:], x_bf)
        for n in range(2):
            layer1(0, n)
        for i in range(2):
            cast_w1(nc.vector.tensor_copy, 1, 2 * i, w1b_raw[i], 0, 128)
        for half in range(2):
            quantise_w1(1, half)
        for n in range(2):
            layer1(1, n)
        for n in range(2):
            quantise(h_codes[0][n], h_scales[0][n], h_bf[0][n])
        for g in range(2):
            prepare_w2(g)
        for n in range(2):
            layer2(0, n)
        for n in range(2):
            quantise(h_codes[1][n], h_scales[1][n], h_bf[1][n])
            layer2(1, n)
            nc.vector.tensor_copy(out_sb[0][n][:], out_ps[0][n][:, 0:P])
            nc.scalar.copy(out_sb[1][n][:], out_ps[1][n][:, 0:P])
            nc.sync.dma_start(out[0:P, P * n : P * n + P], out_sb[0][n][:])
            nc.scalar.dma_start(out[P : 2 * P, P * n : P * n + P], out_sb[1][n][:])
